import numpy as np
import ml_dtypes


def mxq(x, axis, fmt="e4m3"):
    dtype, down = {"e4m3": (ml_dtypes.float8_e4m3fn, 7), "e5m2": (ml_dtypes.float8_e5m2, 14)}[fmt]
    v = np.moveaxis(np.asarray(x, np.float32).astype(ml_dtypes.bfloat16).astype(np.float64), axis, -1)
    blocks = v.reshape(v.shape[:-1] + (-1, 32))
    amax = np.abs(blocks).max(-1, keepdims=True)
    byte = np.maximum(np.where(amax > 0, np.frexp(amax)[1] - 1 + 127, 0) - down, 1)
    scale = np.exp2(byte - 127.0)
    codes = (blocks / scale).astype(np.float32).astype(dtype).astype(np.float64)
    return np.moveaxis((codes * scale).reshape(v.shape), -1, axis)


WIDE = False


def mx_kscale(k):
    if not WIDE:
        return np.ones(k)
    levels = np.array([30, -30])
    if k % 512:
        return np.exp2(np.random.permutation(np.resize(levels, k // 32))).repeat(32)
    a = np.empty((k // 512, 16))
    for p in range(k // 512):
        a[p, :8] = np.random.permutation(np.resize(levels, 8))
        for g in range(8):
            far = levels[np.abs(levels - a[p, g]) >= 10]
            a[p, g + 8] = far[np.random.randint(len(far))]
    return np.exp2(a.ravel()).repeat(32)


def f64(x):
    return np.asarray(x).astype(np.float64)


def striped(idx):
    return np.tile(np.asarray(idx).reshape(-1, 16).T, (8, 1)).astype(np.uint16)


def unstriped(offs):
    return offs[:16].T.reshape(-1).astype(np.int64)


E2M1 = np.array([0.0, 0.5, 1.0, 1.5, 2.0, 3.0, 4.0, 6.0, -0.0, -0.5, -1.0, -1.5, -2.0, -3.0, -4.0, -6.0])


def pack_weight(w, fmt):
    k, n = w.shape
    w = f64(np.asarray(w, np.float32).astype(ml_dtypes.bfloat16)).reshape(k // 32, 32, n)
    amax = np.abs(w).max(1)
    if fmt in ("e4m3", "e5m2"):
        byte = np.frexp(amax)[1] - 1 + 127 - (7 if fmt == "e4m3" else 14)
    else:
        mant, ex = np.frexp(amax / 6.0)
        byte = np.where(mant > 0.5, ex, ex - 1) + 127
    byte = np.clip(np.where(amax > 0, byte, 1), 1, 254)
    scaled = (w * np.exp2(127.0 - byte)[:, None, :]).reshape(k, n).astype(np.float32)
    by_word = np.ascontiguousarray(scaled.reshape(k // 512, 128, 4, n).transpose(0, 1, 3, 2))
    if fmt in ("e4m3", "e5m2"):
        words = by_word.astype(ml_dtypes.float8_e4m3fn if fmt == "e4m3" else ml_dtypes.float8_e5m2).view(np.uint8)
    else:
        c = by_word.astype(ml_dtypes.float4_e2m1fn).view(np.uint8) & 0xF
        words = (c[..., 0::2] | (c[..., 1::2] << 4)).reshape(k // 512, 128, 2 * n)
    return np.ascontiguousarray(words), np.ascontiguousarray(byte.astype(np.uint8).reshape(k // 512, 16, n))


def unpack_weight(words, scales, fmt):
    g, _, n = scales.shape
    words = np.ascontiguousarray(words).reshape(g, 128, n, -1)
    if fmt in ("e4m3", "e5m2"):
        vals = words.view(ml_dtypes.float8_e4m3fn if fmt == "e4m3" else ml_dtypes.float8_e5m2).astype(np.float64)
    else:
        nib = np.empty((g, 128, n, 4), np.uint8)
        nib[..., 0::2] = words & 0xF
        nib[..., 1::2] = words >> 4
        vals = E2M1[nib]
    vals = vals * np.repeat(np.exp2(scales.astype(np.float64) - 127.0), 8, axis=1)[..., None]
    return vals.transpose(0, 1, 3, 2).reshape(g * 512, n)


K, T, J, R, V, C, I, O, N, S = 512, 1024, 256, 512, 1024, 512, 128, 128, 256, 1024


def setup_inputs():
    n = np.random.standard_normal
    idx = np.random.permutation(V)[:R]
    idx2 = np.random.permutation(T)[:J]
    idx3 = np.random.permutation(J)[:I]
    idx4 = np.random.permutation(C)[:I]
    idx5 = np.random.permutation(C)[:O]
    idx6 = np.random.permutation(J)[:O]
    idx7 = np.random.permutation(S)[:N]
    fk = mx_kscale(K)
    fr = mx_kscale(R)
    tr = np.ones(V)
    tr[idx] = fr
    xtp = pack_weight(n((K, T)) / fk[:, None], "e5m2")
    wtp = pack_weight(n((K, V)) * 1 / np.sqrt(K) * fk[:, None] * tr, "e2m1")
    w2p = pack_weight(n((K, R)) * 1 / np.sqrt(K) * fk[:, None], "e4m3")
    vsp = pack_weight(n((R, S)) * 1 / np.sqrt(R) / fr[:, None], "e2m1")
    return {
        "xt_words": xtp[0],
        "xt_scales": xtp[1],
        "wt_words": wtp[0],
        "wt_scales": wtp[1],
        "w2_words": w2p[0],
        "w2_scales": w2p[1],
        "vs_words": vsp[0],
        "vs_scales": vsp[1],
        "offs": striped(idx),
        "offs2": striped(idx2),
        "offs3": striped(idx3),
        "offs4": striped(idx4),
        "offs5": striped(idx5),
        "offs6": striped(idx6),
        "offs7": striped(idx7),
    }


def reference(xt_words, xt_scales, wt_words, wt_scales, w2_words, w2_scales, vs_words, vs_scales, offs, offs2, offs3, offs4, offs5, offs6, offs7):
    idx = unstriped(offs)
    idx2 = unstriped(offs2)
    idx3 = unstriped(offs3)
    idx4 = unstriped(offs4)
    idx5 = unstriped(offs5)
    idx6 = unstriped(offs6)
    idx7 = unstriped(offs7)
    xtu = unpack_weight(xt_words, xt_scales, "e5m2")
    wtu = unpack_weight(wt_words, wt_scales, "e2m1")
    w2u = unpack_weight(w2_words, w2_scales, "e4m3")
    vsu = unpack_weight(vs_words, vs_scales, "e2m1")
    wtidxg = wtu[:, idx]
    xtidx2g = xtu[:, idx2]
    a = wtidxg.T @ xtidx2g
    b = w2u.T @ xtidx2g
    lb = b[:, 0:1]
    la = a[:, 0:1]
    h1 = a[:, idx3] * lb
    pw = np.zeros((R, C))
    pw[:, idx4] = h1
    hid = np.abs(pw[:, idx5] - b[:, idx6] * la)
    vsidx7g = vsu[:, idx7]
    hidq = mxq(hid, 0, "e4m3")
    y = vsidx7g.T @ hidq
    return y

@@ -1,0 +1,154 @@
+from contextlib import ExitStack
+
+import concourse.mybir as mybir
+
+K, T, J, R, V, C, I, O, N, S = 512, 1024, 256, 512, 1024, 512, 128, 128, 256, 1024
+FLOPS = 2 * K * R * J * 2 + 2 * R * N * O
+
+F32 = mybir.dt.float32
+BF16 = mybir.dt.bfloat16
+I32 = mybir.dt.int32
+U32 = mybir.dt.uint32
+U16 = mybir.dt.uint16
+U8 = mybir.dt.uint8
+E4M3 = mybir.dt.float8_e4m3fn_x4
+E5M2 = mybir.dt.float8_e5m2_x4
+E2M1 = mybir.dt.float4_e2m1fn_x4
+ACT = mybir.ActivationFunctionType
+ALU = mybir.AluOpType
+
+P = 128
+PACK = 4
+
+
+def tile_list_leadseats_storeleads_store_plain_kernel(
+    tc, xt_words, xt_scales, wt_words, wt_scales, w2_words, w2_scales, vs_words, vs_scales,
+    offs, offs2, offs3, offs4, offs5, offs6, offs7, out,
+):
+    nc = tc.nc
+    with ExitStack() as ctx:
+        sb = ctx.enter_context(tc.tile_pool(name="sb", bufs=1))
+        ps = ctx.enter_context(tc.psum_pool(name="ps", bufs=1))
+        shared = ctx.enter_context(tc.tile_pool(name="shared", bufs=1))
+
+        def load_list(src, name):
+            lst = sb.tile(list(src.shape), U16, name=name)
+            nc.sync.dma_start(lst[:], src)
+            return lst
+
+        def scale_tile(width, name, engine, pool=sb, **place):
+            plane = pool.tile([P, width], U8, name=name, align_bytes=64, **place)
+            engine.memset(plane[:].bitcast(U32), 0)
+            return plane
+
+        def load_scales(plane, src, queue=nc.sync):
+            for q in range(4):
+                queue.dma_start(plane[32 * q : 32 * q + 4, :].bitcast(I32), src[0, 4 * q : 4 * q + 4, :].bitcast(I32))
+
+        def load_words(src, width, dtype, name, queue=nc.sync):
+            words = sb.tile([P, width], dtype, name=name, align_bytes=64)
+            queue.dma_start(words[:].bitcast(I32), src.bitcast(I32))
+            return words
+
+        xs = scale_tile(T, "xs", nc.vector)
+        w2s = scale_tile(R, "w2s", nc.gpsimd)
+        ws = scale_tile(V, "ws", nc.gpsimd, shared, offset=0)
+        vs = scale_tile(S, "vs", nc.gpsimd)
+        pw = [sb.tile([P, C], F32, name=f"pw{t}") for t in range(PACK)]
+        for t in range(PACK):
+            nc.vector.memset(pw[t][:], 0.0)
+
+        l2 = load_list(offs2, "l2")
+        l1 = load_list(offs, "l1")
+        load_scales(xs, xt_scales)
+        xw = load_words(xt_words[0].rearrange("p n t -> p (n t)"), T, U32, "xw")
+        ww = load_words(wt_words[0], V, U16, "ww")
+        w2w = load_words(w2_words[0].rearrange("p n t -> p (n t)"), R, U32, "w2w", nc.gpsimd)
+        load_scales(w2s, w2_scales)
+        load_scales(ws, wt_scales)
+        l3 = load_list(offs3, "l3")
+        l6 = load_list(offs6, "l6")
+        l4 = load_list(offs4, "l4")
+        l5 = load_list(offs5, "l5")
+        l7 = load_list(offs7, "l7")
+        vw = load_words(vs_words[0], S, U16, "vw", nc.gpsimd)
+        load_scales(vs, vs_scales, nc.gpsimd)
+
+        xsg = sb.tile([P, J], U8, align_bytes=64)
+        xwg = sb.tile([P, J], U32, align_bytes=64)
+        nc.vector.tensor_copy(xsg[:], xs[:].indirect(l2[:]))
+        nc.vector.tensor_copy(xwg[:], xw[:].indirect(l2[:]))
+
+        w2p = sb.tile([P, PACK, P], U32, align_bytes=64)
+        w2sp = sb.tile([P, PACK, P], U8, align_bytes=64)
+        wwg = sb.tile([P, R], U16, align_bytes=64)
+        wwp = sb.tile([P, PACK, P], U16, align_bytes=64)
+        wsg = sb.tile([P, PACK, P], U8, align_bytes=64)
+        nc.scalar.copy(w2p[:].rearrange("p t m -> p m t"), w2w[:].rearrange("p (m t) -> p m t", t=PACK))
+        nc.vector.tensor_copy(wwg[:], ww[:].indirect(l1[:]))
+        nc.vector.tensor_copy(w2sp[:].rearrange("p t m -> p m t"), w2s[:].rearrange("p (m t) -> p m t", t=PACK))
+        nc.vector.tensor_copy(wsg[:].rearrange("p t m -> p m t"), ws[:].indirect(l1[:]))
+        nc.vector.tensor_copy(wwp[:].rearrange("p t m -> p m t"), wwg[:].rearrange("p (m t) -> p m t", t=PACK))
+
+        b_ps = [ps.tile([P, J], F32, name=f"b_ps{t}") for t in range(PACK)]
+        a_ps = [ps.tile([P, J], F32, name=f"a_ps{t}") for t in range(PACK)]
+        b = [sb.tile([P, J], F32, name=f"b{t}") for t in range(PACK)]
+        a = [sb.tile([P, J], F32, name=f"a{t}") for t in range(PACK)]
+        for t in range(PACK):
+            nc.tensor.matmul_mx(b_ps[t][:], lhsT=w2p[:, t, :].bitcast(E4M3), lhsT_scale=w2sp[:, t, :],
+                                rhs=xwg[:].bitcast(E5M2), rhs_scale=xsg[:], start=True, stop=True)
+            nc.scalar.copy(b[t][:], b_ps[t][:])
+        for t in range(PACK):
+            nc.tensor.matmul_mx(a_ps[t][:], lhsT=wwp[:, t, :].bitcast(E2M1), lhsT_scale=wsg[:, t, :],
+                                rhs=xwg[:].bitcast(E5M2), rhs_scale=xsg[:], start=True, stop=True)
+
+        vwg = shared.tile([P, N], U16, align_bytes=64, offset=0)
+        vsg = shared.tile([P, N], U8, align_bytes=64, offset=2 * N)
+        nc.vector.tensor_copy(vwg[:], vw[:].indirect(l7[:]))
+        nc.vector.tensor_copy(vsg[:], vs[:].indirect(l7[:]))
+
+        h1 = [sb.tile([P, I], F32, name=f"h1{t}") for t in range(PACK)]
+        g2 = sb.tile([P, PACK, O], F32)
+        pg = sb.tile([P, PACK, O], F32)
+        diff = sb.tile([P, PACK, O], F32)
+
+        def seats(t):
+            nc.scalar.activation(h1[t][:], a[t][:].indirect(l3[:]), ACT.Copy, scale=b[t][:, 0:1])
+
+        def leads(t):
+            nc.scalar.activation(g2[:, t, :], b[t][:].indirect(l6[:]), ACT.Copy, scale=a[t][:, 0:1])
+
+        nc.scalar.copy(a[0][:], a_ps[0][:])
+        for t in range(PACK):
+            if t + 1 < PACK:
+                nc.scalar.copy(a[t + 1][:], a_ps[t + 1][:])
+            seats(t)
+        leads(0)
+        nc.scalar.activation(pw[3][:].indirect(l4[:]), h1[3][:], ACT.Copy)
+        for t in range(1, PACK):
+            leads(t)
+        nc.scalar.activation(pg[:, 3, :], pw[3][:].indirect(l5[:]), ACT.Copy)
+        for t in range(PACK - 1):
+            nc.vector.tensor_copy(pw[t][:].indirect(l4[:]), h1[t][:])
+        for t in range(PACK - 1):
+            nc.vector.tensor_copy(pg[:, t, :], pw[t][:].indirect(l5[:]))
+        nc.vector.tensor_tensor(diff[:, 0:3, :], pg[:, 0:3, :], g2[:, 0:3, :], ALU.subtract)
+        nc.vector.tensor_tensor(diff[:, 3, :], pg[:, 3, :], g2[:, 3, :], ALU.subtract)
+
+        hid = sb.tile([P, O, PACK], BF16, align_bytes=64)
+        nc.scalar.activation(hid[:], diff[:].rearrange("p t o -> p o t"), ACT.Abs)
+        hq = sb.tile([P, O], U32, align_bytes=64)
+        hs = sb.tile([P, O], U8, align_bytes=64)
+        nc.vector.quantize_mx(out=hq[:].bitcast(E4M3), scales=hs[:], in_=hid[:].rearrange("p o t -> p (o t)"))
+
+        for h in range(N // P):
+            y_ps = ps.tile([P, O], F32, name=f"y_ps{h}", tag=f"b_ps{h}")
+            nc.tensor.matmul_mx(y_ps[:], lhsT=vwg[:, h * P : (h + 1) * P].bitcast(E2M1), lhsT_scale=vsg[:, h * P : (h + 1) * P],
+                                rhs=hq[:].bitcast(E4M3), rhs_scale=hs[:], start=True, stop=True)
+            y = sb.tile([P, O], F32, name=f"y{h}")
+            if h == 0:
+                nc.vector.tensor_copy(y[:], y_ps[:])
+                nc.sync.dma_start(out[h * P : (h + 1) * P, :], y[:])
+            else:
+                nc.scalar.copy(y[:], y_ps[:])
+                nc.scalar.dma_start(out[h * P : (h + 1) * P, :], y[:])

@@ -41,19 +41,19 @@ def tile_list_leadseats_storeleads_store_plain_kernel(
             engine.memset(plane[:].bitcast(U32), 0)
             return plane
 
-        def load_scales(plane, src, queue=nc.sync):
+        def load_scales(plane, src, queues=(nc.sync,) * 4):
             for q in range(4):
-                queue.dma_start(plane[32 * q : 32 * q + 4, :].bitcast(I32), src[0, 4 * q : 4 * q + 4, :].bitcast(I32))
+                queues[q].dma_start(plane[32 * q : 32 * q + 4, :].bitcast(I32), src[0, 4 * q : 4 * q + 4, :].bitcast(I32))
 
         def load_words(src, width, dtype, name, queue=nc.sync):
             words = sb.tile([P, width], dtype, name=name, align_bytes=64)
             queue.dma_start(words[:].bitcast(I32), src.bitcast(I32))
             return words
 
-        xs = scale_tile(T, "xs", nc.vector)
+        xs = scale_tile(T, "xs", nc.gpsimd)
         w2s = scale_tile(R, "w2s", nc.gpsimd)
-        ws = scale_tile(V, "ws", nc.gpsimd, shared, offset=0)
-        vs = scale_tile(S, "vs", nc.gpsimd)
+        ws = scale_tile(V, "ws", nc.vector, shared, offset=0)
+        vs = scale_tile(S, "vs", nc.vector)
         pw = [sb.tile([P, C], F32, name=f"pw{t}") for t in range(PACK)]
         for t in range(PACK):
             nc.vector.memset(pw[t][:], 0.0)
@@ -61,23 +61,22 @@ def tile_list_leadseats_storeleads_store_plain_kernel(
         l2 = load_list(offs2, "l2")
         l1 = load_list(offs, "l1")
         load_scales(xs, xt_scales)
-        xw = load_words(xt_words[0].rearrange("p n t -> p (n t)"), T, U32, "xw")
         ww = load_words(wt_words[0], V, U16, "ww")
+        xw = load_words(xt_words[0].rearrange("p n t -> p (n t)"), T, U32, "xw")
         w2w = load_words(w2_words[0].rearrange("p n t -> p (n t)"), R, U32, "w2w", nc.gpsimd)
-        load_scales(w2s, w2_scales)
+        load_scales(w2s, w2_scales, (nc.sync, nc.sync, nc.sync, nc.gpsimd))
         load_scales(ws, wt_scales)
-        l3 = load_list(offs3, "l3")
-        l6 = load_list(offs6, "l6")
-        l4 = load_list(offs4, "l4")
-        l5 = load_list(offs5, "l5")
         l7 = load_list(offs7, "l7")
         vw = load_words(vs_words[0], S, U16, "vw", nc.gpsimd)
-        load_scales(vs, vs_scales, nc.gpsimd)
+        load_scales(vs, vs_scales)
+        l3 = load_list(offs3, "l3")
+        l4 = load_list(offs4, "l4")
+        l6 = load_list(offs6, "l6")
+        l5 = load_list(offs5, "l5")
 
         xsg = sb.tile([P, J], U8, align_bytes=64)
         xwg = sb.tile([P, J], U32, align_bytes=64)
         nc.vector.tensor_copy(xsg[:], xs[:].indirect(l2[:]))
-        nc.vector.tensor_copy(xwg[:], xw[:].indirect(l2[:]))
 
         w2p = sb.tile([P, PACK, P], U32, align_bytes=64)
         w2sp = sb.tile([P, PACK, P], U8, align_bytes=64)
@@ -86,9 +85,10 @@ def tile_list_leadseats_storeleads_store_plain_kernel(
         wsg = sb.tile([P, PACK, P], U8, align_bytes=64)
         nc.scalar.copy(w2p[:].rearrange("p t m -> p m t"), w2w[:].rearrange("p (m t) -> p m t", t=PACK))
         nc.vector.tensor_copy(wwg[:], ww[:].indirect(l1[:]))
+        nc.vector.tensor_copy(xwg[:], xw[:].indirect(l2[:]))
         nc.vector.tensor_copy(w2sp[:].rearrange("p t m -> p m t"), w2s[:].rearrange("p (m t) -> p m t", t=PACK))
-        nc.vector.tensor_copy(wsg[:].rearrange("p t m -> p m t"), ws[:].indirect(l1[:]))
         nc.vector.tensor_copy(wwp[:].rearrange("p t m -> p m t"), wwg[:].rearrange("p (m t) -> p m t", t=PACK))
+        nc.vector.tensor_copy(wsg[:].rearrange("p t m -> p m t"), ws[:].indirect(l1[:]))
 
         b_ps = [ps.tile([P, J], F32, name=f"b_ps{t}") for t in range(PACK)]
         a_ps = [ps.tile([P, J], F32, name=f"a_ps{t}") for t in range(PACK)]
@@ -108,35 +108,32 @@ def tile_list_leadseats_storeleads_store_plain_kernel(
         nc.vector.tensor_copy(vsg[:], vs[:].indirect(l7[:]))
 
         h1 = [sb.tile([P, I], F32, name=f"h1{t}") for t in range(PACK)]
-        g2 = sb.tile([P, PACK, O], F32)
-        pg = sb.tile([P, PACK, O], F32)
+        g2 = [sb.tile([P, O], F32, name=f"g2{t}", align_bytes=64) for t in range(PACK)]
         diff = sb.tile([P, PACK, O], F32)
 
         def seats(t):
             nc.scalar.activation(h1[t][:], a[t][:].indirect(l3[:]), ACT.Copy, scale=b[t][:, 0:1])
 
         def leads(t):
-            nc.scalar.activation(g2[:, t, :], b[t][:].indirect(l6[:]), ACT.Copy, scale=a[t][:, 0:1])
+            nc.scalar.activation(g2[t][:], b[t][:].indirect(l6[:]), ACT.Copy, scale=a[t][:, 0:1])
 
         nc.scalar.copy(a[0][:], a_ps[0][:])
         for t in range(PACK):
             if t + 1 < PACK:
                 nc.scalar.copy(a[t + 1][:], a_ps[t + 1][:])
             seats(t)
+        for t in range(PACK - 1):
+            nc.vector.tensor_copy(pw[t][:].indirect(l4[:]), h1[t][:])
         leads(0)
         nc.scalar.activation(pw[3][:].indirect(l4[:]), h1[3][:], ACT.Copy)
         for t in range(1, PACK):
             leads(t)
-        nc.scalar.activation(pg[:, 3, :], pw[3][:].indirect(l5[:]), ACT.Copy)
-        for t in range(PACK - 1):
-            nc.vector.tensor_copy(pw[t][:].indirect(l4[:]), h1[t][:])
-        for t in range(PACK - 1):
-            nc.vector.tensor_copy(pg[:, t, :], pw[t][:].indirect(l5[:]))
-        nc.vector.tensor_tensor(diff[:, 0:3, :], pg[:, 0:3, :], g2[:, 0:3, :], ALU.subtract)
-        nc.vector.tensor_tensor(diff[:, 3, :], pg[:, 3, :], g2[:, 3, :], ALU.subtract)
+        for t in range(PACK):
+            nc.vector.tensor_tensor(diff[:, t, :], pw[t][:].indirect(l5[:]), g2[t][:], ALU.subtract)
 
         hid = sb.tile([P, O, PACK], BF16, align_bytes=64)
-        nc.scalar.activation(hid[:], diff[:].rearrange("p t o -> p o t"), ACT.Abs)
+        for u in range(2):
+            nc.scalar.activation(hid[:, :, 2 * u : 2 * u + 2], diff[:, 2 * u : 2 * u + 2, :].rearrange("p t o -> p o t"), ACT.Abs)
         hq = sb.tile([P, O], U32, align_bytes=64)
         hs = sb.tile([P, O], U8, align_bytes=64)
         nc.vector.quantize_mx(out=hq[:].bitcast(E4M3), scales=hs[:], in_=hid[:].rearrange("p o t -> p (o t)"))

@@ -50,8 +50,14 @@ def tile_list_leadseats_storeleads_store_plain_kernel(
             queue.dma_start(words[:].bitcast(I32), src.bitcast(I32))
             return words
 
+        def dealt(dst, src, run):
+            return (
+                dst[:].rearrange("p t (g i) -> p g t i", i=run),
+                src[:].rearrange("p (g i t) -> p g t i", i=run, t=PACK),
+            )
+
         xs = scale_tile(T, "xs", nc.gpsimd)
-        w2s = scale_tile(R, "w2s", nc.gpsimd)
+        w2s = scale_tile(R, "w2s", nc.gpsimd, shared, offset=V)
         ws = scale_tile(V, "ws", nc.vector, shared, offset=0)
         vs = scale_tile(S, "vs", nc.vector)
         pw = [sb.tile([P, C], F32, name=f"pw{t}") for t in range(PACK)]
@@ -59,17 +65,17 @@ def tile_list_leadseats_storeleads_store_plain_kernel(
             nc.vector.memset(pw[t][:], 0.0)
 
         l2 = load_list(offs2, "l2")
-        l1 = load_list(offs, "l1")
         load_scales(xs, xt_scales)
+        l1 = load_list(offs, "l1")
         ww = load_words(wt_words[0], V, U16, "ww")
         xw = load_words(xt_words[0].rearrange("p n t -> p (n t)"), T, U32, "xw")
         w2w = load_words(w2_words[0].rearrange("p n t -> p (n t)"), R, U32, "w2w", nc.gpsimd)
-        load_scales(w2s, w2_scales, (nc.sync, nc.sync, nc.sync, nc.gpsimd))
-        load_scales(ws, wt_scales)
+        load_scales(w2s, w2_scales)
+        load_scales(ws, wt_scales, (nc.sync, nc.sync, nc.sync, nc.gpsimd))
         l7 = load_list(offs7, "l7")
         vw = load_words(vs_words[0], S, U16, "vw", nc.gpsimd)
-        load_scales(vs, vs_scales)
         l3 = load_list(offs3, "l3")
+        load_scales(vs, vs_scales)
         l4 = load_list(offs4, "l4")
         l6 = load_list(offs6, "l6")
         l5 = load_list(offs5, "l5")
@@ -81,13 +87,13 @@ def tile_list_leadseats_storeleads_store_plain_kernel(
         w2p = sb.tile([P, PACK, P], U32, align_bytes=64)
         w2sp = sb.tile([P, PACK, P], U8, align_bytes=64)
         wwg = sb.tile([P, R], U16, align_bytes=64)
-        wwp = sb.tile([P, PACK, P], U16, align_bytes=64)
+        wwp = shared.tile([P, PACK, P], U16, align_bytes=64, offset=V)
         wsg = sb.tile([P, PACK, P], U8, align_bytes=64)
-        nc.scalar.copy(w2p[:].rearrange("p t m -> p m t"), w2w[:].rearrange("p (m t) -> p m t", t=PACK))
+        nc.scalar.copy(*dealt(w2p, w2w, 4))
         nc.vector.tensor_copy(wwg[:], ww[:].indirect(l1[:]))
         nc.vector.tensor_copy(xwg[:], xw[:].indirect(l2[:]))
-        nc.vector.tensor_copy(w2sp[:].rearrange("p t m -> p m t"), w2s[:].rearrange("p (m t) -> p m t", t=PACK))
-        nc.vector.tensor_copy(wwp[:].rearrange("p t m -> p m t"), wwg[:].rearrange("p (m t) -> p m t", t=PACK))
+        nc.vector.tensor_copy(*dealt(w2sp, w2s, 16))
+        nc.vector.tensor_copy(*dealt(wwp, wwg, 8))
         nc.vector.tensor_copy(wsg[:].rearrange("p t m -> p m t"), ws[:].indirect(l1[:]))
 
         b_ps = [ps.tile([P, J], F32, name=f"b_ps{t}") for t in range(PACK)]

@@ -59,7 +59,7 @@ def tile_list_leadseats_storeleads_store_plain_kernel(
         xs = scale_tile(T, "xs", nc.gpsimd)
         w2s = scale_tile(R, "w2s", nc.gpsimd, shared, offset=V)
         ws = scale_tile(V, "ws", nc.vector, shared, offset=0)
-        vs = scale_tile(S, "vs", nc.vector)
+        vs = scale_tile(S, "vs", nc.vector, shared, offset=2 * V)
         pw = [sb.tile([P, C], F32, name=f"pw{t}") for t in range(PACK)]
         for t in range(PACK):
             nc.vector.memset(pw[t][:], 0.0)
@@ -75,10 +75,10 @@ def tile_list_leadseats_storeleads_store_plain_kernel(
         l7 = load_list(offs7, "l7")
         vw = load_words(vs_words[0], S, U16, "vw", nc.gpsimd)
         l3 = load_list(offs3, "l3")
-        load_scales(vs, vs_scales)
         l4 = load_list(offs4, "l4")
         l6 = load_list(offs6, "l6")
         l5 = load_list(offs5, "l5")
+        load_scales(vs, vs_scales)
 
         xsg = sb.tile([P, J], U8, align_bytes=64)
         xwg = sb.tile([P, J], U32, align_bytes=64)
@@ -109,13 +109,11 @@ def tile_list_leadseats_storeleads_store_plain_kernel(
                                 rhs=xwg[:].bitcast(E5M2), rhs_scale=xsg[:], start=True, stop=True)
 
         vwg = shared.tile([P, N], U16, align_bytes=64, offset=0)
-        vsg = shared.tile([P, N], U8, align_bytes=64, offset=2 * N)
         nc.vector.tensor_copy(vwg[:], vw[:].indirect(l7[:]))
-        nc.vector.tensor_copy(vsg[:], vs[:].indirect(l7[:]))
 
         h1 = [sb.tile([P, I], F32, name=f"h1{t}") for t in range(PACK)]
         g2 = [sb.tile([P, O], F32, name=f"g2{t}", align_bytes=64) for t in range(PACK)]
-        diff = sb.tile([P, PACK, O], F32)
+        diff = [sb.tile([P, 2, O], F32, name=f"diff{u}", align_bytes=64) for u in range(2)]
 
         def seats(t):
             nc.scalar.activation(h1[t][:], a[t][:].indirect(l3[:]), ACT.Copy, scale=b[t][:, 0:1])
@@ -124,10 +122,13 @@ def tile_list_leadseats_storeleads_store_plain_kernel(
             nc.scalar.activation(g2[t][:], b[t][:].indirect(l6[:]), ACT.Copy, scale=a[t][:, 0:1])
 
         nc.scalar.copy(a[0][:], a_ps[0][:])
-        for t in range(PACK):
-            if t + 1 < PACK:
-                nc.scalar.copy(a[t + 1][:], a_ps[t + 1][:])
-            seats(t)
+        nc.vector.tensor_copy(a[1][:], a_ps[1][:])
+        seats(0)
+        nc.scalar.copy(a[2][:], a_ps[2][:])
+        seats(1)
+        nc.scalar.copy(a[3][:], a_ps[3][:])
+        seats(2)
+        seats(3)
         for t in range(PACK - 1):
             nc.vector.tensor_copy(pw[t][:].indirect(l4[:]), h1[t][:])
         leads(0)
@@ -135,13 +136,15 @@ def tile_list_leadseats_storeleads_store_plain_kernel(
         for t in range(1, PACK):
             leads(t)
         for t in range(PACK):
-            nc.vector.tensor_tensor(diff[:, t, :], pw[t][:].indirect(l5[:]), g2[t][:], ALU.subtract)
+            nc.vector.tensor_tensor(diff[t // 2][:, t % 2, :], pw[t][:].indirect(l5[:]), g2[t][:], ALU.subtract)
 
         hid = sb.tile([P, O, PACK], BF16, align_bytes=64)
         for u in range(2):
-            nc.scalar.activation(hid[:, :, 2 * u : 2 * u + 2], diff[:, 2 * u : 2 * u + 2, :].rearrange("p t o -> p o t"), ACT.Abs)
+            nc.scalar.activation(hid[:, :, 2 * u : 2 * u + 2], diff[u][:].rearrange("p t o -> p o t"), ACT.Abs)
+        vsg = sb.tile([P, N], U8, tag="diff0", align_bytes=64)
+        nc.vector.tensor_copy(vsg[:], vs[:].indirect(l7[:]))
         hq = sb.tile([P, O], U32, align_bytes=64)
-        hs = sb.tile([P, O], U8, align_bytes=64)
+        hs = shared.tile([P, O], U8, align_bytes=64, offset=2 * V)
         nc.vector.quantize_mx(out=hq[:].bitcast(E4M3), scales=hs[:], in_=hid[:].rearrange("p o t -> p (o t)"))
 
         for h in range(N // P):

from contextlib import ExitStack

import concourse.mybir as mybir

K, T, J, R, V, C, I, O, N, S = 512, 1024, 256, 512, 1024, 512, 128, 128, 256, 1024
FLOPS = 2 * K * R * J * 2 + 2 * R * N * O

F32 = mybir.dt.float32
BF16 = mybir.dt.bfloat16
I32 = mybir.dt.int32
U32 = mybir.dt.uint32
U16 = mybir.dt.uint16
U8 = mybir.dt.uint8
E4M3 = mybir.dt.float8_e4m3fn_x4
E5M2 = mybir.dt.float8_e5m2_x4
E2M1 = mybir.dt.float4_e2m1fn_x4
ACT = mybir.ActivationFunctionType
ALU = mybir.AluOpType

P = 128
PACK = 4


def tile_list_leadseats_storeleads_store_plain_kernel(
    tc, xt_words, xt_scales, wt_words, wt_scales, w2_words, w2_scales, vs_words, vs_scales,
    offs, offs2, offs3, offs4, offs5, offs6, offs7, out,
):
    nc = tc.nc
    with ExitStack() as ctx:
        sb = ctx.enter_context(tc.tile_pool(name="sb", bufs=1))
        ps = ctx.enter_context(tc.psum_pool(name="ps", bufs=1))
        shared = ctx.enter_context(tc.tile_pool(name="shared", bufs=1))

        def load_list(src, name):
            lst = sb.tile(list(src.shape), U16, name=name)
            nc.sync.dma_start(lst[:], src)
            return lst

        def scale_tile(width, name, engine, pool=sb, **place):
            plane = pool.tile([P, width], U8, name=name, align_bytes=64, **place)
            engine.memset(plane[:].bitcast(U32), 0)
            return plane

        def load_scales(plane, src, queues=(nc.sync,) * 4):
            for q in range(4):
                queues[q].dma_start(plane[32 * q : 32 * q + 4, :].bitcast(I32), src[0, 4 * q : 4 * q + 4, :].bitcast(I32))

        def load_words(src, width, dtype, name, queue=nc.sync):
            words = sb.tile([P, width], dtype, name=name, align_bytes=64)
            queue.dma_start(words[:].bitcast(I32), src.bitcast(I32))
            return words

        def dealt(dst, src, run):
            return (
                dst[:].rearrange("p t (g i) -> p g t i", i=run),
                src[:].rearrange("p (g i t) -> p g t i", i=run, t=PACK),
            )

        xs = scale_tile(T, "xs", nc.gpsimd)
        w2s = scale_tile(R, "w2s", nc.gpsimd, shared, offset=V)
        ws = scale_tile(V, "ws", nc.vector, shared, offset=0)
        vs = scale_tile(S, "vs", nc.vector, shared, offset=2 * V)
        pw = [sb.tile([P, C], F32, name=f"pw{t}") for t in range(PACK)]
        for t in range(PACK):
            nc.vector.memset(pw[t][:], 0.0)

        l2 = load_list(offs2, "l2")
        load_scales(xs, xt_scales)
        l1 = load_list(offs, "l1")
        ww = load_words(wt_words[0], V, U16, "ww")
        xw = load_words(xt_words[0].rearrange("p n t -> p (n t)"), T, U32, "xw")
        w2w = load_words(w2_words[0].rearrange("p n t -> p (n t)"), R, U32, "w2w", nc.gpsimd)
        load_scales(w2s, w2_scales)
        load_scales(ws, wt_scales, (nc.sync, nc.sync, nc.sync, nc.gpsimd))
        l7 = load_list(offs7, "l7")
        vw = load_words(vs_words[0], S, U16, "vw", nc.gpsimd)
        l3 = load_list(offs3, "l3")
        l4 = load_list(offs4, "l4")
        l6 = load_list(offs6, "l6")
        l5 = load_list(offs5, "l5")
        load_scales(vs, vs_scales)

        xsg = sb.tile([P, J], U8, align_bytes=64)
        xwg = sb.tile([P, J], U32, align_bytes=64)
        nc.vector.tensor_copy(xsg[:], xs[:].indirect(l2[:]))

        w2p = sb.tile([P, PACK, P], U32, align_bytes=64)
        w2sp = sb.tile([P, PACK, P], U8, align_bytes=64)
        wwg = sb.tile([P, R], U16, align_bytes=64)
        wwp = shared.tile([P, PACK, P], U16, align_bytes=64, offset=V)
        wsg = sb.tile([P, PACK, P], U8, align_bytes=64)
        nc.scalar.copy(*dealt(w2p, w2w, 4))
        nc.vector.tensor_copy(wwg[:], ww[:].indirect(l1[:]))
        nc.vector.tensor_copy(xwg[:], xw[:].indirect(l2[:]))
        nc.vector.tensor_copy(*dealt(w2sp, w2s, 16))
        nc.vector.tensor_copy(*dealt(wwp, wwg, 8))
        nc.vector.tensor_copy(wsg[:].rearrange("p t m -> p m t"), ws[:].indirect(l1[:]))

        b_ps = [ps.tile([P, J], F32, name=f"b_ps{t}") for t in range(PACK)]
        a_ps = [ps.tile([P, J], F32, name=f"a_ps{t}") for t in range(PACK)]
        b = [sb.tile([P, J], F32, name=f"b{t}") for t in range(PACK)]
        a = [sb.tile([P, J], F32, name=f"a{t}") for t in range(PACK)]
        for t in range(PACK):
            nc.tensor.matmul_mx(b_ps[t][:], lhsT=w2p[:, t, :].bitcast(E4M3), lhsT_scale=w2sp[:, t, :],
                                rhs=xwg[:].bitcast(E5M2), rhs_scale=xsg[:], start=True, stop=True)
            nc.scalar.copy(b[t][:], b_ps[t][:])
        for t in range(PACK):
            nc.tensor.matmul_mx(a_ps[t][:], lhsT=wwp[:, t, :].bitcast(E2M1), lhsT_scale=wsg[:, t, :],
                                rhs=xwg[:].bitcast(E5M2), rhs_scale=xsg[:], start=True, stop=True)

        vwg = shared.tile([P, N], U16, align_bytes=64, offset=0)
        nc.vector.tensor_copy(vwg[:], vw[:].indirect(l7[:]))

        h1 = [sb.tile([P, I], F32, name=f"h1{t}") for t in range(PACK)]
        g2 = [sb.tile([P, O], F32, name=f"g2{t}", align_bytes=64) for t in range(PACK)]
        diff = [sb.tile([P, 2, O], F32, name=f"diff{u}", align_bytes=64) for u in range(2)]

        def seats(t):
            nc.scalar.activation(h1[t][:], a[t][:].indirect(l3[:]), ACT.Copy, scale=b[t][:, 0:1])

        def leads(t):
            nc.scalar.activation(g2[t][:], b[t][:].indirect(l6[:]), ACT.Copy, scale=a[t][:, 0:1])

        nc.scalar.copy(a[0][:], a_ps[0][:])
        nc.vector.tensor_copy(a[1][:], a_ps[1][:])
        seats(0)
        nc.scalar.copy(a[2][:], a_ps[2][:])
        seats(1)
        nc.scalar.copy(a[3][:], a_ps[3][:])
        seats(2)
        seats(3)
        for t in range(PACK - 1):
            nc.vector.tensor_copy(pw[t][:].indirect(l4[:]), h1[t][:])
        leads(0)
        nc.scalar.activation(pw[3][:].indirect(l4[:]), h1[3][:], ACT.Copy)
        for t in range(1, PACK):
            leads(t)
        for t in range(PACK):
            nc.vector.tensor_tensor(diff[t // 2][:, t % 2, :], pw[t][:].indirect(l5[:]), g2[t][:], ALU.subtract)

        hid = sb.tile([P, O, PACK], BF16, align_bytes=64)
        for u in range(2):
            nc.scalar.activation(hid[:, :, 2 * u : 2 * u + 2], diff[u][:].rearrange("p t o -> p o t"), ACT.Abs)
        vsg = sb.tile([P, N], U8, tag="diff0", align_bytes=64)
        nc.vector.tensor_copy(vsg[:], vs[:].indirect(l7[:]))
        hq = sb.tile([P, O], U32, align_bytes=64)
        hs = shared.tile([P, O], U8, align_bytes=64, offset=2 * V)
        nc.vector.quantize_mx(out=hq[:].bitcast(E4M3), scales=hs[:], in_=hid[:].rearrange("p o t -> p (o t)"))

        for h in range(N // P):
            y_ps = ps.tile([P, O], F32, name=f"y_ps{h}", tag=f"b_ps{h}")
            nc.tensor.matmul_mx(y_ps[:], lhsT=vwg[:, h * P : (h + 1) * P].bitcast(E2M1), lhsT_scale=vsg[:, h * P : (h + 1) * P],
                                rhs=hq[:].bitcast(E4M3), rhs_scale=hs[:], start=True, stop=True)
            y = sb.tile([P, O], F32, name=f"y{h}")
            if h == 0:
                nc.vector.tensor_copy(y[:], y_ps[:])
                nc.sync.dma_start(out[h * P : (h + 1) * P, :], y[:])
            else:
                nc.scalar.copy(y[:], y_ps[:])
                nc.scalar.dma_start(out[h * P : (h + 1) * P, :], y[:])
